import numpy as np
import ml_dtypes


def mxq(x, axis, fmt="e4m3"):
    dtype, down = {"e4m3": (ml_dtypes.float8_e4m3fn, 7), "e5m2": (ml_dtypes.float8_e5m2, 14)}[fmt]
    v = np.moveaxis(np.asarray(x, np.float32).astype(ml_dtypes.bfloat16).astype(np.float64), axis, -1)
    blocks = v.reshape(v.shape[:-1] + (-1, 32))
    amax = np.abs(blocks).max(-1, keepdims=True)
    byte = np.maximum(np.where(amax > 0, np.frexp(amax)[1] - 1 + 127, 0) - down, 1)
    scale = np.exp2(byte - 127.0)
    codes = (blocks / scale).astype(np.float32).astype(dtype).astype(np.float64)
    return np.moveaxis((codes * scale).reshape(v.shape), -1, axis)


WIDE = False


def mx_kscale(k):
    if not WIDE:
        return np.ones(k)
    levels = np.array([10, -10, 5, -5, 0])
    if k % 512:
        return np.exp2(np.random.permutation(np.resize(levels, k // 32))).repeat(32)
    a = np.empty((k // 512, 16))
    for p in range(k // 512):
        a[p, :8] = np.random.permutation(np.resize(levels, 8))
        for g in range(8):
            far = levels[np.abs(levels - a[p, g]) >= 10]
            a[p, g + 8] = far[np.random.randint(len(far))]
    return np.exp2(a.ravel()).repeat(32)


def f64(x):
    return np.asarray(x).astype(np.float64)


def striped(idx):
    return np.tile(np.asarray(idx).reshape(-1, 16).T, (8, 1)).astype(np.uint16)


def unstriped(offs):
    return offs[:16].T.reshape(-1).astype(np.int64)


E2M1 = np.array([0.0, 0.5, 1.0, 1.5, 2.0, 3.0, 4.0, 6.0, -0.0, -0.5, -1.0, -1.5, -2.0, -3.0, -4.0, -6.0])


def pack_weight(w, fmt):
    k, n = w.shape
    w = f64(np.asarray(w, np.float32).astype(ml_dtypes.bfloat16)).reshape(k // 32, 32, n)
    amax = np.abs(w).max(1)
    if fmt == "e4m3":
        byte = np.frexp(amax)[1] - 1 + 127 - 7
    else:
        mant, ex = np.frexp(amax / 6.0)
        byte = np.where(mant > 0.5, ex, ex - 1) + 127
    byte = np.clip(np.where(amax > 0, byte, 1), 1, 254)
    scaled = (w * np.exp2(127.0 - byte)[:, None, :]).reshape(k, n).astype(np.float32)
    by_word = np.ascontiguousarray(scaled.reshape(k // 512, 128, 4, n).transpose(0, 1, 3, 2))
    if fmt == "e4m3":
        words = by_word.astype(ml_dtypes.float8_e4m3fn).view(np.uint8)
    else:
        c = by_word.astype(ml_dtypes.float4_e2m1fn).view(np.uint8) & 0xF
        words = (c[..., 0::2] | (c[..., 1::2] << 4)).reshape(k // 512, 128, 2 * n)
    return np.ascontiguousarray(words), np.ascontiguousarray(byte.astype(np.uint8).reshape(k // 512, 16, n))


def unpack_weight(words, scales, fmt):
    g, _, n = scales.shape
    words = np.ascontiguousarray(words).reshape(g, 128, n, -1)
    if fmt == "e4m3":
        vals = words.view(ml_dtypes.float8_e4m3fn).astype(np.float64)
    else:
        nib = np.empty((g, 128, n, 4), np.uint8)
        nib[..., 0::2] = words & 0xF
        nib[..., 1::2] = words >> 4
        vals = E2M1[nib]
    vals = vals * np.repeat(np.exp2(scales.astype(np.float64) - 127.0), 8, axis=1)[..., None]
    return vals.transpose(0, 1, 3, 2).reshape(g * 512, n)


def bf(x):
    return np.asarray(x, np.float32).astype(ml_dtypes.bfloat16)


def planes(Y):
    r, m = Y.shape
    b = f64(bf(Y)).reshape(r // 32, 32, m)
    amax = np.abs(b).max(1)
    byte = np.clip(np.where(amax > 0, np.frexp(amax)[1] - 1 + 127 - 7, 1), 1, 254)
    codes = (b * np.exp2(127.0 - byte)[:, None, :]).reshape(r, m).astype(np.float32).astype(ml_dtypes.float8_e4m3fn).view(np.uint8)
    words = codes.reshape(r // 512, 128, 4, m).transpose(0, 1, 3, 2)
    return np.ascontiguousarray(words), np.ascontiguousarray(byte.astype(np.uint8).reshape(r // 512, 16, m))


K, T, J, R, N = 512, 1024, 128, 512, 512


def setup_inputs():
    n = np.random.standard_normal
    idx = np.random.permutation(T)[:J]
    fk = mx_kscale(K)
    fr = mx_kscale(R)
    xqp = pack_weight(n((K, T)) / fk[:, None], "e2m1")
    w1p = pack_weight(n((K, R)) * 1 / np.sqrt(K) * fk[:, None] * fr, "e4m3")
    wxp = pack_weight(n((R, N)) * 1 / np.sqrt(R) / fr[:, None], "e2m1")
    wbp = pack_weight(n((R, N)) * 1 / np.sqrt(R) / fr[:, None], "e4m3")
    return {
        "xq_words": xqp[0],
        "xq_scales": xqp[1],
        "w1_words": w1p[0],
        "w1_scales": w1p[1],
        "wx_words": wxp[0],
        "wx_scales": wxp[1],
        "wb_words": wbp[0],
        "wb_scales": wbp[1],
        "offs": striped(idx),
    }


def reference(xq_words, xq_scales, w1_words, w1_scales, wx_words, wx_scales, wb_words, wb_scales, offs):
    idx = unstriped(offs)
    xqu = unpack_weight(xq_words, xq_scales, "e2m1")
    w1u = unpack_weight(w1_words, w1_scales, "e4m3")
    wxu = unpack_weight(wx_words, wx_scales, "e2m1")
    wbu = unpack_weight(wb_words, wb_scales, "e4m3")
    a = w1u.T @ xqu
    hid = np.maximum(a, 0.0)
    hidq = mxq(hid, 0, "e4m3")
    e = wxu.T @ hidq
    hididxq = mxq(hid[:, idx], 0, "e4m3")
    p = wbu.T @ hididxq
    d = 4.0 * np.maximum(p, 0.0)
    dp = np.zeros((N, T))
    dp[:, idx] = d
    y = e + dp
    words, scales = planes(y)
    return y, words, scales

@@ -1,0 +1,192 @@
+from contextlib import ExitStack
+
+import concourse.mybir as mybir
+
+K, T, J, R, N = 512, 1024, 128, 512, 512
+FLOPS = 2 * K * R * T + 2 * R * N * T + 2 * R * N * J
+
+F32 = mybir.dt.float32
+BF16 = mybir.dt.bfloat16
+I32 = mybir.dt.int32
+U16 = mybir.dt.uint16
+U8 = mybir.dt.uint8
+FP8X4 = mybir.dt.float8_e4m3fn_x4
+FP4X4 = mybir.dt.float4_e2m1fn_x4
+RELU = mybir.ActivationFunctionType.Relu
+ADD = mybir.AluOpType.add
+MAX = mybir.AluOpType.max
+
+P = 128
+PACK = 4
+QUADS = 4
+HALF = 512
+CHUNK = 256
+CHUNKS = T // CHUNK
+VECTOR_BANKS = (3, 6)
+
+
+def interleave(copy, dst, src):
+    copy(out=dst.rearrange("p (c i) t -> p c t i", i=4), in_=src.rearrange("p t (c i) -> p c t i", i=4))
+
+
+def deal(nc, dst, src, run):
+    nc.vector.tensor_copy(out=dst.rearrange("p t (c i) -> p c t i", i=run), in_=src.rearrange("p (c i) t -> p c t i", i=run))
+
+
+def tile_list_stay_or_leave_pl_kernel(tc, xq_words, xq_scales, w1_words, w1_scales, wx_words, wx_scales,
+                                          wb_words, wb_scales, offs, out_0, out_1, out_2):
+    nc = tc.nc
+    with ExitStack() as ctx:
+        keep = ctx.enter_context(tc.tile_pool(name="keep", bufs=1))
+        psum = ctx.enter_context(tc.psum_pool(name="psum", bufs=1))
+
+        def sbuf(name, shape, dtype, tag=None):
+            return keep.tile(shape, dtype, name=name, tag=tag or name, align_bytes=64)
+
+        def bank(name, index, shape):
+            return psum.tile(shape, F32, name=name, tag="bank%d" % index)
+
+        offsets = keep.tile([P, J // 16], U16, name="offsets")
+
+        w1_raw = sbuf("w1_raw", [P, R], I32)
+        w1s_raw = sbuf("w1s_raw", [P, R], U8)
+        x_codes = [sbuf("x_codes%d" % h, [P, 2 * HALF], U8) for h in range(2)]
+        x_scales = sbuf("x_scales", [P, T], U8)
+        wb_raw = sbuf("wb_raw", [P, N], I32)
+        wx_raw = sbuf("wx_raw", [P, N], U16)
+        s2_raw = sbuf("s2_raw", [P, N], U8)
+
+        def load_plane(queue, plane, scales, q):
+            rows = scales[0].bitcast(I32)[4 * q : 4 * q + 4, :]
+            queue.dma_start(out=plane[:].bitcast(I32)[32 * q : 32 * q + 32, :], in_=rows.partition_broadcast(8))
+
+        def load_rows(plane, first, scales, q):
+            rows = scales[0].bitcast(I32)[4 * q : 4 * q + 4, :]
+            nc.sync.dma_start(out=plane[:].bitcast(I32)[32 * q + first : 32 * q + first + 4, :], in_=rows)
+
+        def words(ap):
+            return ap[0].rearrange("p n t -> p (n t)").bitcast(I32)
+
+        x_words = xq_words[0].bitcast(I32)
+        load_plane(nc.sync, w1s_raw, w1_scales, 0)
+        load_plane(nc.scalar, w1s_raw, w1_scales, 1)
+        nc.sync.dma_start(out=w1_raw[:], in_=words(w1_words))
+        nc.scalar.dma_start(out=x_codes[0][:].bitcast(I32), in_=x_words[:, : HALF // 2])
+        load_plane(nc.sync, w1s_raw, w1_scales, 2)
+        load_plane(nc.scalar, w1s_raw, w1_scales, 3)
+        load_plane(nc.sync, x_scales, xq_scales, 0)
+        load_plane(nc.scalar, x_scales, xq_scales, 1)
+        load_plane(nc.sync, x_scales, xq_scales, 2)
+        load_plane(nc.sync, x_scales, xq_scales, 3)
+        nc.sync.dma_start(out=x_codes[1][:].bitcast(I32), in_=x_words[:, HALF // 2 :])
+        nc.sync.dma_start(offsets[:], offs)
+        nc.sync.dma_start(out=wb_raw[:], in_=words(wb_words))
+        nc.sync.dma_start(out=wx_raw[:].bitcast(I32), in_=wx_words[0].bitcast(I32))
+        nc.vector.memset(s2_raw[:].bitcast(I32), 0)
+        for q in range(QUADS):
+            load_rows(s2_raw, 4, wb_scales, q)
+        for q in range(QUADS):
+            load_rows(s2_raw, 0, wx_scales, q)
+
+        pages = [sbuf("page%d" % t, [P, T], F32) for t in range(PACK)]
+        for t in range(PACK):
+            nc.vector.memset(pages[t][:], 0.0)
+
+        w1_first = sbuf("w1_first", [P, 1, P], I32)
+        w1s_first = sbuf("w1s_first", [P, 1, P], U8)
+        w1_rest = sbuf("w1_rest", [P, PACK - 1, P], I32)
+        w1s_rest = sbuf("w1s_rest", [P, PACK - 1, P], U8)
+        w1_by_t = w1_raw[:].rearrange("p (m t) -> p m t", t=PACK)
+        w1s_by_t = w1s_raw[:].rearrange("p (m t) -> p m t", t=PACK)
+        deal(nc, w1s_first[:], w1s_by_t[:, :, :1], 16)
+        deal(nc, w1_first[:], w1_by_t[:, :, :1], 4)
+        deal(nc, w1s_rest[:], w1s_by_t[:, :, 1:], 16)
+        deal(nc, w1_rest[:], w1_by_t[:, :, 1:], 4)
+        w1_codes = [w1_first[:, 0, :]] + [w1_rest[:, t, :] for t in range(PACK - 1)]
+        w1_planes = [w1s_first[:, 0, :]] + [w1s_rest[:, t, :] for t in range(PACK - 1)]
+
+        wb_codes = sbuf("wb_codes", [P, PACK, P], I32)
+        wx_codes = sbuf("wx_codes", [P, PACK, P], U16)
+        s2 = sbuf("s2", [P, PACK, P], U8)
+
+        hid = sbuf("hid", [P, PACK * T], F32)
+        picked = sbuf("picked", [P, J, PACK], BF16, tag="first_rounded")
+        for t in range(PACK):
+            for h in range(2):
+                b = 2 * t + h
+                a = bank("a%d" % b, b, [P, HALF])
+                nc.tensor.matmul_mx(out=a[:], lhsT=w1_codes[t].bitcast(FP8X4), lhsT_scale=w1_planes[t],
+                                    rhs=x_codes[h][:].bitcast(FP4X4), rhs_scale=x_scales[:, h * HALF : (h + 1) * HALF],
+                                    start=True, stop=True)
+                dst = hid[:, b * HALF : (b + 1) * HALF]
+                if b in VECTOR_BANKS:
+                    nc.vector.tensor_scalar_max(dst, a[:], 0.0)
+                else:
+                    nc.scalar.activation(dst, a[:], RELU)
+            nc.vector.tensor_copy(picked[:, :, t], hid[:, t * T : (t + 1) * T].indirect(offsets[:]))
+
+        deal(nc, wb_codes[:], wb_raw[:].rearrange("p (m t) -> p m t", t=PACK), 4)
+        deal(nc, s2[:], s2_raw[:].rearrange("p (m t) -> p m t", t=PACK), 16)
+        deal(nc, wx_codes[:], wx_raw[:].rearrange("p (m t) -> p m t", t=PACK), 8)
+
+        picked_codes = sbuf("picked_codes", [P, J], I32)
+        picked_scales = sbuf("picked_scales", [P, J], U8)
+        nc.vector.quantize_mx(out=picked_codes[:].bitcast(FP8X4), scales=picked_scales[:],
+                              in_=picked[:].rearrange("p j t -> p (j t)"))
+        p_first = bank("p_first", 0, [P, 1, J])
+        p_rest = bank("p_rest", 1, [P, PACK - 1, J])
+        p_slices = [p_first[:, 0, :]] + [p_rest[:, t, :] for t in range(PACK - 1)]
+        for t in range(PACK):
+            nc.tensor.matmul_mx(out=p_slices[t], lhsT=wb_codes[:, t, :].bitcast(FP8X4), lhsT_scale=s2[4:, t, :],
+                                rhs=picked_codes[:].bitcast(FP8X4), rhs_scale=picked_scales[:], start=True, stop=True)
+        d_first = sbuf("d_first", [P, 1, J], F32)
+        d_rest = sbuf("d_rest", [P, PACK - 1, J], F32)
+        nc.scalar.activation(d_first[:], p_first[:], RELU, scale=4.0)
+        nc.scalar.activation(d_rest[:], p_rest[:], RELU, scale=4.0)
+        d_slices = [d_first[:, 0, :]] + [d_rest[:, t, :] for t in range(PACK - 1)]
+
+        hid_by_t = hid[:].rearrange("p (t c) -> p t c", t=PACK)
+        e_banks = []
+
+        def exit_product(c):
+            hb = sbuf("hid_bf%d" % c, [P, CHUNK, PACK], BF16, tag="first_rounded" if c == 0 else None)
+            src = hid_by_t[:, :, c * CHUNK : (c + 1) * CHUNK]
+            if c == 0:
+                interleave(nc.vector.tensor_copy, hb[:], src)
+            else:
+                for u in range(2):
+                    cols = slice(u * CHUNK // 2, (u + 1) * CHUNK // 2)
+                    interleave(nc.scalar.copy, hb[:, cols, :], src[:, :, cols])
+            codes = sbuf("hid_codes%d" % c, [P, CHUNK], I32)
+            scales = sbuf("hid_scales%d" % c, [P, CHUNK], U8)
+            nc.vector.quantize_mx(out=codes[:].bitcast(FP8X4), scales=scales[:], in_=hb[:].rearrange("p c t -> p (c t)"))
+            for u in range(2):
+                e = bank("e%d_%d" % (c, u), (2 + 2 * c + u) % 8, [P, 2, CHUNK])
+                e_banks.append(e)
+                for v in range(2):
+                    t = 2 * u + v
+                    nc.tensor.matmul_mx(out=e[:, v, :], lhsT=wx_codes[:, t, :].bitcast(FP4X4), lhsT_scale=s2[:, t, :],
+                                        rhs=codes[:].bitcast(FP8X4), rhs_scale=scales[:], start=True, stop=True)
+
+        for c in range(CHUNKS):
+            exit_product(c)
+            nc.vector.tensor_copy(pages[c][:].indirect(offsets[:]), d_slices[c])
+
+        y_scales = sbuf("y_scales", [P, T], U8)
+        out_rows = out_0.rearrange("(p t) c -> p t c", t=PACK)
+        out_words = words(out_1)
+        for c in range(CHUNKS):
+            cols = slice(c * CHUNK, (c + 1) * CHUNK)
+            y = sbuf("y%d" % c, [P, PACK, CHUNK], F32)
+            for t in range(PACK):
+                nc.vector.tensor_tensor(y[:, t, :], e_banks[2 * c + t // 2][:, t % 2, :], pages[t][:, cols], ADD)
+            nc.sync.dma_start(out=out_rows[:, :, cols], in_=y[:])
+            yb = sbuf("y_bf%d" % c, [P, CHUNK, PACK], BF16)
+            interleave(nc.vector.tensor_copy if c == CHUNKS - 1 else nc.scalar.copy, yb[:], y[:])
+            y_codes = sbuf("y_codes%d" % c, [P, CHUNK], I32)
+            nc.vector.quantize_mx(out=y_codes[:].bitcast(FP8X4), scales=y_scales[:, cols], in_=yb[:].rearrange("p c t -> p (c t)"))
+            nc.sync.dma_start(out=out_words[:, cols], in_=y_codes[:])
+        out_scales = out_2[0].bitcast(I32)
+        for q in range(QUADS):
+            queue = nc.scalar if q % 2 == 0 else nc.sync
+            queue.dma_start(out=out_scales[4 * q : 4 * q + 4, :], in_=y_scales[:].bitcast(I32)[32 * q : 32 * q + 4, :])

@@ -50,47 +50,43 @@ def tile_list_stay_or_leave_pl_kernel(tc, xq_words, xq_scales, w1_words, w1_scal
 
         w1_raw = sbuf("w1_raw", [P, R], I32)
         w1s_raw = sbuf("w1s_raw", [P, R], U8)
-        x_codes = [sbuf("x_codes%d" % h, [P, 2 * HALF], U8) for h in range(2)]
+        x_codes = sbuf("x_codes", [P, 2 * T], U8)
         x_scales = sbuf("x_scales", [P, T], U8)
         wb_raw = sbuf("wb_raw", [P, N], I32)
         wx_raw = sbuf("wx_raw", [P, N], U16)
-        s2_raw = sbuf("s2_raw", [P, N], U8)
+        wbs_raw = sbuf("wbs_raw", [P, N], U8)
+        wxs_raw = sbuf("wxs_raw", [P, N], U8)
+
+        pages = [sbuf("page%d" % t, [P, T], F32) for t in range(PACK)]
+        for t in range(PACK):
+            nc.vector.memset(pages[t][:], 0.0)
 
         def load_plane(queue, plane, scales, q):
             rows = scales[0].bitcast(I32)[4 * q : 4 * q + 4, :]
             queue.dma_start(out=plane[:].bitcast(I32)[32 * q : 32 * q + 32, :], in_=rows.partition_broadcast(8))
 
-        def load_rows(plane, first, scales, q):
-            rows = scales[0].bitcast(I32)[4 * q : 4 * q + 4, :]
-            nc.sync.dma_start(out=plane[:].bitcast(I32)[32 * q + first : 32 * q + first + 4, :], in_=rows)
-
         def words(ap):
             return ap[0].rearrange("p n t -> p (n t)").bitcast(I32)
 
-        x_words = xq_words[0].bitcast(I32)
         load_plane(nc.sync, w1s_raw, w1_scales, 0)
         load_plane(nc.scalar, w1s_raw, w1_scales, 1)
         nc.sync.dma_start(out=w1_raw[:], in_=words(w1_words))
-        nc.scalar.dma_start(out=x_codes[0][:].bitcast(I32), in_=x_words[:, : HALF // 2])
+        nc.scalar.dma_start(out=x_codes[:].bitcast(I32), in_=xq_words[0].bitcast(I32))
         load_plane(nc.sync, w1s_raw, w1_scales, 2)
         load_plane(nc.scalar, w1s_raw, w1_scales, 3)
-        load_plane(nc.sync, x_scales, xq_scales, 0)
-        load_plane(nc.scalar, x_scales, xq_scales, 1)
-        load_plane(nc.sync, x_scales, xq_scales, 2)
-        load_plane(nc.sync, x_scales, xq_scales, 3)
-        nc.sync.dma_start(out=x_codes[1][:].bitcast(I32), in_=x_words[:, HALF // 2 :])
-        nc.sync.dma_start(offsets[:], offs)
+        for q in range(QUADS):
+            if q == 2:
+                warm = sbuf("warm", [P, 1], F32)
+                nc.scalar.activation(warm[:], pages[0][:, :1], RELU)
+            load_plane(nc.scalar if q % 2 else nc.sync, x_scales, xq_scales, q)
         nc.sync.dma_start(out=wb_raw[:], in_=words(wb_words))
-        nc.sync.dma_start(out=wx_raw[:].bitcast(I32), in_=wx_words[0].bitcast(I32))
-        nc.vector.memset(s2_raw[:].bitcast(I32), 0)
+        nc.scalar.dma_start(out=wx_raw[:].bitcast(I32), in_=wx_words[0].bitcast(I32))
+        nc.sync.dma_start(offsets[:], offs)
         for q in range(QUADS):
-            load_rows(s2_raw, 4, wb_scales, q)
+            load_plane(nc.sync if q % 2 else nc.scalar, wbs_raw, wb_scales, q)
         for q in range(QUADS):
-            load_rows(s2_raw, 0, wx_scales, q)
+            load_plane(nc.sync if q else nc.scalar, wxs_raw, wx_scales, q)
 
-        pages = [sbuf("page%d" % t, [P, T], F32) for t in range(PACK)]
-        for t in range(PACK):
-            nc.vector.memset(pages[t][:], 0.0)
 
         w1_first = sbuf("w1_first", [P, 1, P], I32)
         w1s_first = sbuf("w1s_first", [P, 1, P], U8)
@@ -107,7 +103,8 @@ def tile_list_stay_or_leave_pl_kernel(tc, xq_words, xq_scales, w1_words, w1_scal
 
         wb_codes = sbuf("wb_codes", [P, PACK, P], I32)
         wx_codes = sbuf("wx_codes", [P, PACK, P], U16)
-        s2 = sbuf("s2", [P, PACK, P], U8)
+        wb_planes = sbuf("wb_planes", [P, PACK, P], U8)
+        wx_planes = sbuf("wx_planes", [P, PACK, P], U8)
 
         hid = sbuf("hid", [P, PACK * T], F32)
         picked = sbuf("picked", [P, J, PACK], BF16, tag="first_rounded")
@@ -116,7 +113,7 @@ def tile_list_stay_or_leave_pl_kernel(tc, xq_words, xq_scales, w1_words, w1_scal
                 b = 2 * t + h
                 a = bank("a%d" % b, b, [P, HALF])
                 nc.tensor.matmul_mx(out=a[:], lhsT=w1_codes[t].bitcast(FP8X4), lhsT_scale=w1_planes[t],
-                                    rhs=x_codes[h][:].bitcast(FP4X4), rhs_scale=x_scales[:, h * HALF : (h + 1) * HALF],
+                                    rhs=x_codes[:, 2 * h * HALF : 2 * (h + 1) * HALF].bitcast(FP4X4), rhs_scale=x_scales[:, h * HALF : (h + 1) * HALF],
                                     start=True, stop=True)
                 dst = hid[:, b * HALF : (b + 1) * HALF]
                 if b in VECTOR_BANKS:
@@ -126,8 +123,9 @@ def tile_list_stay_or_leave_pl_kernel(tc, xq_words, xq_scales, w1_words, w1_scal
             nc.vector.tensor_copy(picked[:, :, t], hid[:, t * T : (t + 1) * T].indirect(offsets[:]))
 
         deal(nc, wb_codes[:], wb_raw[:].rearrange("p (m t) -> p m t", t=PACK), 4)
-        deal(nc, s2[:], s2_raw[:].rearrange("p (m t) -> p m t", t=PACK), 16)
+        deal(nc, wb_planes[:], wbs_raw[:].rearrange("p (m t) -> p m t", t=PACK), 16)
         deal(nc, wx_codes[:], wx_raw[:].rearrange("p (m t) -> p m t", t=PACK), 8)
+        deal(nc, wx_planes[:], wxs_raw[:].rearrange("p (m t) -> p m t", t=PACK), 16)
 
         picked_codes = sbuf("picked_codes", [P, J], I32)
         picked_scales = sbuf("picked_scales", [P, J], U8)
@@ -137,7 +135,7 @@ def tile_list_stay_or_leave_pl_kernel(tc, xq_words, xq_scales, w1_words, w1_scal
         p_rest = bank("p_rest", 1, [P, PACK - 1, J])
         p_slices = [p_first[:, 0, :]] + [p_rest[:, t, :] for t in range(PACK - 1)]
         for t in range(PACK):
-            nc.tensor.matmul_mx(out=p_slices[t], lhsT=wb_codes[:, t, :].bitcast(FP8X4), lhsT_scale=s2[4:, t, :],
+            nc.tensor.matmul_mx(out=p_slices[t], lhsT=wb_codes[:, t, :].bitcast(FP8X4), lhsT_scale=wb_planes[:, t, :],
                                 rhs=picked_codes[:].bitcast(FP8X4), rhs_scale=picked_scales[:], start=True, stop=True)
         d_first = sbuf("d_first", [P, 1, J], F32)
         d_rest = sbuf("d_rest", [P, PACK - 1, J], F32)
@@ -149,7 +147,7 @@ def tile_list_stay_or_leave_pl_kernel(tc, xq_words, xq_scales, w1_words, w1_scal
         e_banks = []
 
         def exit_product(c):
-            hb = sbuf("hid_bf%d" % c, [P, CHUNK, PACK], BF16, tag="first_rounded" if c == 0 else None)
+            hb = sbuf("hid_bf%d" % c, [P, CHUNK, PACK], BF16, tag=["first_rounded", None, "picked_codes", "picked_scales"][c])
             src = hid_by_t[:, :, c * CHUNK : (c + 1) * CHUNK]
             if c == 0:
                 interleave(nc.vector.tensor_copy, hb[:], src)
@@ -165,7 +163,7 @@ def tile_list_stay_or_leave_pl_kernel(tc, xq_words, xq_scales, w1_words, w1_scal
                 e_banks.append(e)
                 for v in range(2):
                     t = 2 * u + v
-                    nc.tensor.matmul_mx(out=e[:, v, :], lhsT=wx_codes[:, t, :].bitcast(FP4X4), lhsT_scale=s2[:, t, :],
+                    nc.tensor.matmul_mx(out=e[:, v, :], lhsT=wx_codes[:, t, :].bitcast(FP4X4), lhsT_scale=wx_planes[:, t, :],
                                         rhs=codes[:].bitcast(FP8X4), rhs_scale=scales[:], start=True, stop=True)
 
         for c in range(CHUNKS):

@@ -26,7 +26,7 @@ VECTOR_BANKS = (3, 6)
 
 
 def interleave(copy, dst, src):
-    copy(out=dst.rearrange("p (c i) t -> p c t i", i=4), in_=src.rearrange("p t (c i) -> p c t i", i=4))
+    copy(out=dst, in_=src.rearrange("p t c -> p c t"))
 
 
 def deal(nc, dst, src, run):
@@ -59,7 +59,7 @@ def tile_list_stay_or_leave_pl_kernel(tc, xq_words, xq_scales, w1_words, w1_scal
 
         pages = [sbuf("page%d" % t, [P, T], F32) for t in range(PACK)]
         for t in range(PACK):
-            nc.vector.memset(pages[t][:], 0.0)
+            (nc.gpsimd if t == 3 else nc.vector).memset(pages[t][:].bitcast(I32), 0)
 
         def load_plane(queue, plane, scales, q):
             rows = scales[0].bitcast(I32)[4 * q : 4 * q + 4, :]
@@ -68,25 +68,25 @@ def tile_list_stay_or_leave_pl_kernel(tc, xq_words, xq_scales, w1_words, w1_scal
         def words(ap):
             return ap[0].rearrange("p n t -> p (n t)").bitcast(I32)
 
-        load_plane(nc.sync, w1s_raw, w1_scales, 0)
-        load_plane(nc.scalar, w1s_raw, w1_scales, 1)
+        queues = (nc.sync, nc.scalar)
+        for q in range(QUADS):
+            load_plane(queues[q % 2], w1s_raw, w1_scales, q)
         nc.sync.dma_start(out=w1_raw[:], in_=words(w1_words))
         nc.scalar.dma_start(out=x_codes[:].bitcast(I32), in_=xq_words[0].bitcast(I32))
-        load_plane(nc.sync, w1s_raw, w1_scales, 2)
-        load_plane(nc.scalar, w1s_raw, w1_scales, 3)
         for q in range(QUADS):
             if q == 2:
                 warm = sbuf("warm", [P, 1], F32)
                 nc.scalar.activation(warm[:], pages[0][:, :1], RELU)
-            load_plane(nc.scalar if q % 2 else nc.sync, x_scales, xq_scales, q)
+            load_plane(queues[q % 2], x_scales, xq_scales, q)
+        for q in range(2):
+            load_plane(queues[q % 2], wbs_raw, wb_scales, q)
         nc.sync.dma_start(out=wb_raw[:], in_=words(wb_words))
         nc.scalar.dma_start(out=wx_raw[:].bitcast(I32), in_=wx_words[0].bitcast(I32))
         nc.sync.dma_start(offsets[:], offs)
+        for q in range(2, QUADS):
+            load_plane(queues[1 - q % 2], wbs_raw, wb_scales, q)
         for q in range(QUADS):
-            load_plane(nc.sync if q % 2 else nc.scalar, wbs_raw, wb_scales, q)
-        for q in range(QUADS):
-            load_plane(nc.sync if q else nc.scalar, wxs_raw, wx_scales, q)
-
+            load_plane(queues[1 - q % 2], wxs_raw, wx_scales, q)
 
         w1_first = sbuf("w1_first", [P, 1, P], I32)
         w1s_first = sbuf("w1s_first", [P, 1, P], U8)
@@ -137,54 +137,93 @@ def tile_list_stay_or_leave_pl_kernel(tc, xq_words, xq_scales, w1_words, w1_scal
         for t in range(PACK):
             nc.tensor.matmul_mx(out=p_slices[t], lhsT=wb_codes[:, t, :].bitcast(FP8X4), lhsT_scale=wb_planes[:, t, :],
                                 rhs=picked_codes[:].bitcast(FP8X4), rhs_scale=picked_scales[:], start=True, stop=True)
-        d_first = sbuf("d_first", [P, 1, J], F32)
-        d_rest = sbuf("d_rest", [P, PACK - 1, J], F32)
-        nc.scalar.activation(d_first[:], p_first[:], RELU, scale=4.0)
-        nc.scalar.activation(d_rest[:], p_rest[:], RELU, scale=4.0)
-        d_slices = [d_first[:, 0, :]] + [d_rest[:, t, :] for t in range(PACK - 1)]
-
+        d = [sbuf("d%d" % t, [P, J], F32) for t in range(PACK)]
         hid_by_t = hid[:].rearrange("p (t c) -> p t c", t=PACK)
-        e_banks = []
+        hid_bf = [sbuf("hid_bf%d" % c, [P, CHUNK, PACK], BF16, tag=tag)
+                  for c, tag in enumerate(("first_rounded", None, "picked_codes", "picked_scales"))]
+
+        def round_hid(copy, c, first, count):
+            interleave(copy, hid_bf[c][:, first : first + count, :],
+                       hid_by_t[:, :, c * CHUNK + first : c * CHUNK + first + count])
+
+        def further(t):
+            nc.scalar.activation(d[t][:], p_slices[t], RELU, scale=4.0)
+
+        piece = CHUNK // 2
+        round_hid(nc.scalar.copy, 1, 0, piece)
+        round_hid(nc.scalar.copy, 1, piece, piece)
+        further(0)
+        further(1)
+        round_hid(nc.scalar.copy, 2, 0, CHUNK)
+        further(2)
+        round_hid(nc.scalar.copy, 3, 0, piece)
+        further(3)
+        round_hid(nc.scalar.copy, 3, piece, piece)
+        round_hid(nc.vector.tensor_copy, 0, 0, CHUNK)
+
+        e_low = [bank("e_low%d" % t, 2 + t, [P, 2, CHUNK]) for t in range(PACK)]
+        e_high = [bank("e_high%d" % u, (6 + u) % 8, [P, 2, CHUNK]) for u in range(PACK)]
+
+        def e_part(c, t):
+            return e_low[t][:, c, :] if c < 2 else e_high[2 * (c - 2) + t // 2][:, t % 2, :]
 
         def exit_product(c):
-            hb = sbuf("hid_bf%d" % c, [P, CHUNK, PACK], BF16, tag=["first_rounded", None, "picked_codes", "picked_scales"][c])
-            src = hid_by_t[:, :, c * CHUNK : (c + 1) * CHUNK]
-            if c == 0:
-                interleave(nc.vector.tensor_copy, hb[:], src)
-            else:
-                for u in range(2):
-                    cols = slice(u * CHUNK // 2, (u + 1) * CHUNK // 2)
-                    interleave(nc.scalar.copy, hb[:, cols, :], src[:, :, cols])
             codes = sbuf("hid_codes%d" % c, [P, CHUNK], I32)
             scales = sbuf("hid_scales%d" % c, [P, CHUNK], U8)
-            nc.vector.quantize_mx(out=codes[:].bitcast(FP8X4), scales=scales[:], in_=hb[:].rearrange("p c t -> p (c t)"))
-            for u in range(2):
-                e = bank("e%d_%d" % (c, u), (2 + 2 * c + u) % 8, [P, 2, CHUNK])
-                e_banks.append(e)
-                for v in range(2):
-                    t = 2 * u + v
-                    nc.tensor.matmul_mx(out=e[:, v, :], lhsT=wx_codes[:, t, :].bitcast(FP4X4), lhsT_scale=wx_planes[:, t, :],
-                                        rhs=codes[:].bitcast(FP8X4), rhs_scale=scales[:], start=True, stop=True)
+            nc.vector.quantize_mx(out=codes[:].bitcast(FP8X4), scales=scales[:], in_=hid_bf[c][:].rearrange("p c t -> p (c t)"))
+            for t in range(PACK):
+                nc.tensor.matmul_mx(out=e_part(c, t), lhsT=wx_codes[:, t, :].bitcast(FP4X4), lhsT_scale=wx_planes[:, t, :],
+                                    rhs=codes[:].bitcast(FP8X4), rhs_scale=scales[:], start=True, stop=True)
 
-        for c in range(CHUNKS):
-            exit_product(c)
-            nc.vector.tensor_copy(pages[c][:].indirect(offsets[:]), d_slices[c])
-
-        y_scales = sbuf("y_scales", [P, T], U8)
         out_rows = out_0.rearrange("(p t) c -> p t c", t=PACK)
         out_words = words(out_1)
-        for c in range(CHUNKS):
+        y_low = sbuf("y_low", [P, PACK * HALF], F32)
+        y_low_by_t = y_low[:].rearrange("p (t c) -> p t c", t=PACK)
+        y_high = [sbuf("y_high%d" % c, [P, PACK, CHUNK], F32) for c in range(2)]
+        y_scales = sbuf("y_scales", [P, T], U8)
+
+        def place(t):
+            nc.vector.tensor_copy(pages[t][:].indirect(offsets[:]), d[t][:])
+
+        def add_low(t, width):
+            e = e_low[t][:].rearrange("p c j -> p (c j)")
+            for first in range(0, HALF, width):
+                nc.vector.tensor_tensor(y_low[:, t * HALF + first : t * HALF + first + width], e[:, first : first + width],
+                                        pages[t][:, first : first + width], ADD)
+            nc.sync.dma_start(out=out_rows[:, t, :HALF], in_=y_low[:, t * HALF : (t + 1) * HALF])
+
+        def add_high(c):
             cols = slice(c * CHUNK, (c + 1) * CHUNK)
-            y = sbuf("y%d" % c, [P, PACK, CHUNK], F32)
             for t in range(PACK):
-                nc.vector.tensor_tensor(y[:, t, :], e_banks[2 * c + t // 2][:, t % 2, :], pages[t][:, cols], ADD)
-            nc.sync.dma_start(out=out_rows[:, :, cols], in_=y[:])
-            yb = sbuf("y_bf%d" % c, [P, CHUNK, PACK], BF16)
-            interleave(nc.vector.tensor_copy if c == CHUNKS - 1 else nc.scalar.copy, yb[:], y[:])
+                nc.vector.tensor_tensor(y_high[c - 2][:, t, :], e_part(c, t), pages[t][:, cols], ADD)
+            nc.sync.dma_start(out=out_rows[:, :, cols], in_=y_high[c - 2][:])
+
+        def hand_on(c):
+            cols = slice(c * CHUNK, (c + 1) * CHUNK)
+            y_bf = sbuf("y_bf%d" % c, [P, CHUNK, PACK], BF16)
+            interleave(nc.vector.tensor_copy if c == CHUNKS - 1 else nc.scalar.copy, y_bf[:],
+                       y_low_by_t[:, :, cols] if c < 2 else y_high[c - 2][:])
             y_codes = sbuf("y_codes%d" % c, [P, CHUNK], I32)
-            nc.vector.quantize_mx(out=y_codes[:].bitcast(FP8X4), scales=y_scales[:, cols], in_=yb[:].rearrange("p c t -> p (c t)"))
+            nc.vector.quantize_mx(out=y_codes[:].bitcast(FP8X4), scales=y_scales[:, cols], in_=y_bf[:].rearrange("p c t -> p (c t)"))
             nc.sync.dma_start(out=out_words[:, cols], in_=y_codes[:])
+
+        exit_product(0)
+        exit_product(1)
+        place(0)
+        place(1)
+        add_low(0, HALF)
+        place(2)
+        add_low(1, HALF)
+        exit_product(2)
+        add_low(2, HALF)
+        place(3)
+        add_low(3, CHUNK)
+        exit_product(3)
+        add_high(2)
+        hand_on(0)
+        add_high(3)
+        for c in range(1, CHUNKS):
+            hand_on(c)
         out_scales = out_2[0].bitcast(I32)
         for q in range(QUADS):
-            queue = nc.scalar if q % 2 == 0 else nc.sync
-            queue.dma_start(out=out_scales[4 * q : 4 * q + 4, :], in_=y_scales[:].bitcast(I32)[32 * q : 32 * q + 4, :])
+            queues[1 - q % 2].dma_start(out=out_scales[4 * q : 4 * q + 4, :], in_=y_scales[:].bitcast(I32)[32 * q : 32 * q + 4, :])

@@ -22,11 +22,12 @@ QUADS = 4
 HALF = 512
 CHUNK = 256
 CHUNKS = T // CHUNK
-VECTOR_BANKS = (3, 6)
+LAST_ON_SCALAR = 96
+VECTOR_BANKS = (1, 3, 6)
 
 
 def interleave(copy, dst, src):
-    copy(out=dst, in_=src.rearrange("p t c -> p c t"))
+    copy(out=dst.rearrange("p (c i) t -> p c t i", i=4), in_=src.rearrange("p t (c i) -> p c t i", i=4))
 
 
 def deal(nc, dst, src, run):
@@ -54,8 +55,8 @@ def tile_list_stay_or_leave_pl_kernel(tc, xq_words, xq_scales, w1_words, w1_scal
         x_scales = sbuf("x_scales", [P, T], U8)
         wb_raw = sbuf("wb_raw", [P, N], I32)
         wx_raw = sbuf("wx_raw", [P, N], U16)
-        wbs_raw = sbuf("wbs_raw", [P, N], U8)
-        wxs_raw = sbuf("wxs_raw", [P, N], U8)
+        second_raw = sbuf("second_raw", [P, N], U8)
+        nc.vector.memset(second_raw[:].bitcast(I32), 0)
 
         pages = [sbuf("page%d" % t, [P, T], F32) for t in range(PACK)]
         for t in range(PACK):
@@ -64,6 +65,10 @@ def tile_list_stay_or_leave_pl_kernel(tc, xq_words, xq_scales, w1_words, w1_scal
         def load_plane(queue, plane, scales, q):
             rows = scales[0].bitcast(I32)[4 * q : 4 * q + 4, :]
             queue.dma_start(out=plane[:].bitcast(I32)[32 * q : 32 * q + 32, :], in_=rows.partition_broadcast(8))
+
+        def load_rows(queue, first, scales, q):
+            rows = scales[0].bitcast(I32)[4 * q : 4 * q + 4, :]
+            queue.dma_start(out=second_raw[:].bitcast(I32)[32 * q + first : 32 * q + first + 4, :], in_=rows)
 
         def words(ap):
             return ap[0].rearrange("p n t -> p (n t)").bitcast(I32)
@@ -78,15 +83,13 @@ def tile_list_stay_or_leave_pl_kernel(tc, xq_words, xq_scales, w1_words, w1_scal
                 warm = sbuf("warm", [P, 1], F32)
                 nc.scalar.activation(warm[:], pages[0][:, :1], RELU)
             load_plane(queues[q % 2], x_scales, xq_scales, q)
-        for q in range(2):
-            load_plane(queues[q % 2], wbs_raw, wb_scales, q)
+        nc.sync.dma_start(offsets[:], offs)
         nc.sync.dma_start(out=wb_raw[:], in_=words(wb_words))
         nc.scalar.dma_start(out=wx_raw[:].bitcast(I32), in_=wx_words[0].bitcast(I32))
-        nc.sync.dma_start(offsets[:], offs)
-        for q in range(2, QUADS):
-            load_plane(queues[1 - q % 2], wbs_raw, wb_scales, q)
         for q in range(QUADS):
-            load_plane(queues[1 - q % 2], wxs_raw, wx_scales, q)
+            load_rows(queues[1 - q % 2], 4, wb_scales, q)
+        for q in range(QUADS):
+            load_rows(queues[1 - q % 2], 0, wx_scales, q)
 
         w1_first = sbuf("w1_first", [P, 1, P], I32)
         w1s_first = sbuf("w1s_first", [P, 1, P], U8)
@@ -103,11 +106,11 @@ def tile_list_stay_or_leave_pl_kernel(tc, xq_words, xq_scales, w1_words, w1_scal
 
         wb_codes = sbuf("wb_codes", [P, PACK, P], I32)
         wx_codes = sbuf("wx_codes", [P, PACK, P], U16)
-        wb_planes = sbuf("wb_planes", [P, PACK, P], U8)
-        wx_planes = sbuf("wx_planes", [P, PACK, P], U8)
+        second_planes = sbuf("second_planes", [P, PACK, P], U8)
 
         hid = sbuf("hid", [P, PACK * T], F32)
-        picked = sbuf("picked", [P, J, PACK], BF16, tag="first_rounded")
+        low_bf = sbuf("low_bf", [P, HALF, PACK], BF16)
+        picked = low_bf[:, :J, :]
         for t in range(PACK):
             for h in range(2):
                 b = 2 * t + h
@@ -123,107 +126,121 @@ def tile_list_stay_or_leave_pl_kernel(tc, xq_words, xq_scales, w1_words, w1_scal
             nc.vector.tensor_copy(picked[:, :, t], hid[:, t * T : (t + 1) * T].indirect(offsets[:]))
 
         deal(nc, wb_codes[:], wb_raw[:].rearrange("p (m t) -> p m t", t=PACK), 4)
-        deal(nc, wb_planes[:], wbs_raw[:].rearrange("p (m t) -> p m t", t=PACK), 16)
         deal(nc, wx_codes[:], wx_raw[:].rearrange("p (m t) -> p m t", t=PACK), 8)
-        deal(nc, wx_planes[:], wxs_raw[:].rearrange("p (m t) -> p m t", t=PACK), 16)
+        deal(nc, second_planes[:], second_raw[:].rearrange("p (m t) -> p m t", t=PACK), 16)
 
         picked_codes = sbuf("picked_codes", [P, J], I32)
         picked_scales = sbuf("picked_scales", [P, J], U8)
         nc.vector.quantize_mx(out=picked_codes[:].bitcast(FP8X4), scales=picked_scales[:],
-                              in_=picked[:].rearrange("p j t -> p (j t)"))
+                              in_=picked.rearrange("p j t -> p (j t)"))
         p_first = bank("p_first", 0, [P, 1, J])
         p_rest = bank("p_rest", 1, [P, PACK - 1, J])
         p_slices = [p_first[:, 0, :]] + [p_rest[:, t, :] for t in range(PACK - 1)]
         for t in range(PACK):
-            nc.tensor.matmul_mx(out=p_slices[t], lhsT=wb_codes[:, t, :].bitcast(FP8X4), lhsT_scale=wb_planes[:, t, :],
+            nc.tensor.matmul_mx(out=p_slices[t], lhsT=wb_codes[:, t, :].bitcast(FP8X4), lhsT_scale=second_planes[4:, t, :],
                                 rhs=picked_codes[:].bitcast(FP8X4), rhs_scale=picked_scales[:], start=True, stop=True)
         d = [sbuf("d%d" % t, [P, J], F32) for t in range(PACK)]
         hid_by_t = hid[:].rearrange("p (t c) -> p t c", t=PACK)
-        hid_bf = [sbuf("hid_bf%d" % c, [P, CHUNK, PACK], BF16, tag=tag)
-                  for c, tag in enumerate(("first_rounded", None, "picked_codes", "picked_scales"))]
 
-        def round_hid(copy, c, first, count):
-            interleave(copy, hid_bf[c][:, first : first + count, :],
-                       hid_by_t[:, :, c * CHUNK + first : c * CHUNK + first + count])
+        def round_hid(copy, dst, first, count):
+            interleave(copy, dst, hid_by_t[:, :, first : first + count])
 
-        def further(t):
+        def quantise(name, rounded, width, tag=None):
+            codes = sbuf(name + "_codes", [P, width], I32, tag=tag)
+            scales = sbuf(name + "_scales", [P, width], U8)
+            nc.vector.quantize_mx(out=codes[:].bitcast(FP8X4), scales=scales[:], in_=rounded[:].rearrange("p c t -> p (c t)"))
+            return codes, scales
+
+        def exit_product(e_slices, codes, scales):
+            for t in range(PACK):
+                nc.tensor.matmul_mx(out=e_slices[t], lhsT=wx_codes[:, t, :].bitcast(FP4X4), lhsT_scale=second_planes[:, t, :],
+                                    rhs=codes[:].bitcast(FP8X4), rhs_scale=scales[:], start=True, stop=True)
+
+        for first in range(J, HALF, J):
+            round_hid(nc.scalar.copy, low_bf[:, first : first + J, :], first, J)
+        for t in range(PACK):
             nc.scalar.activation(d[t][:], p_slices[t], RELU, scale=4.0)
+        round_hid(nc.vector.tensor_copy, picked, 0, J)
 
-        piece = CHUNK // 2
-        round_hid(nc.scalar.copy, 1, 0, piece)
-        round_hid(nc.scalar.copy, 1, piece, piece)
-        further(0)
-        further(1)
-        round_hid(nc.scalar.copy, 2, 0, CHUNK)
-        further(2)
-        round_hid(nc.scalar.copy, 3, 0, piece)
-        further(3)
-        round_hid(nc.scalar.copy, 3, piece, piece)
-        round_hid(nc.vector.tensor_copy, 0, 0, CHUNK)
-
-        e_low = [bank("e_low%d" % t, 2 + t, [P, 2, CHUNK]) for t in range(PACK)]
+        e_low = [bank("e_low%d" % t, 2 + t, [P, HALF]) for t in range(PACK)]
         e_high = [bank("e_high%d" % u, (6 + u) % 8, [P, 2, CHUNK]) for u in range(PACK)]
 
         def e_part(c, t):
-            return e_low[t][:, c, :] if c < 2 else e_high[2 * (c - 2) + t // 2][:, t % 2, :]
+            return e_low[t][:, c * CHUNK : (c + 1) * CHUNK] if c < 2 else e_high[2 * (c - 2) + t // 2][:, t % 2, :]
 
-        def exit_product(c):
-            codes = sbuf("hid_codes%d" % c, [P, CHUNK], I32)
-            scales = sbuf("hid_scales%d" % c, [P, CHUNK], U8)
-            nc.vector.quantize_mx(out=codes[:].bitcast(FP8X4), scales=scales[:], in_=hid_bf[c][:].rearrange("p c t -> p (c t)"))
-            for t in range(PACK):
-                nc.tensor.matmul_mx(out=e_part(c, t), lhsT=wx_codes[:, t, :].bitcast(FP4X4), lhsT_scale=wx_planes[:, t, :],
-                                    rhs=codes[:].bitcast(FP8X4), rhs_scale=scales[:], start=True, stop=True)
+        def round_high(c, tag):
+            rounded = sbuf("hid_bf%d" % c, [P, CHUNK, PACK], BF16, tag=tag)
+            for first in range(0, CHUNK, J):
+                round_hid(nc.scalar.copy, rounded[:, first : first + J, :], c * CHUNK + first, J)
+            return rounded
+
+        def exit_high(c, rounded):
+            exit_product([e_part(c, t) for t in range(PACK)], *quantise("hid%d" % c, rounded, CHUNK))
 
         out_rows = out_0.rearrange("(p t) c -> p t c", t=PACK)
         out_words = words(out_1)
-        y_low = sbuf("y_low", [P, PACK * HALF], F32)
-        y_low_by_t = y_low[:].rearrange("p (t c) -> p t c", t=PACK)
-        y_high = [sbuf("y_high%d" % c, [P, PACK, CHUNK], F32) for c in range(2)]
+        y_low = sbuf("y_low", [P, PACK, HALF], F32)
+        y_codes = sbuf("y_codes", [P, T], I32)
         y_scales = sbuf("y_scales", [P, T], U8)
 
         def place(t):
             nc.vector.tensor_copy(pages[t][:].indirect(offsets[:]), d[t][:])
 
-        def add_low(t, width):
-            e = e_low[t][:].rearrange("p c j -> p (c j)")
-            for first in range(0, HALF, width):
-                nc.vector.tensor_tensor(y_low[:, t * HALF + first : t * HALF + first + width], e[:, first : first + width],
-                                        pages[t][:, first : first + width], ADD)
-            nc.sync.dma_start(out=out_rows[:, t, :HALF], in_=y_low[:, t * HALF : (t + 1) * HALF])
+        def add_low_on_gpsimd(t):
+            e = sbuf("e_copy%d" % t, [P, HALF], F32)
+            nc.scalar.copy(e[:], e_low[t][:])
+            nc.gpsimd.tensor_tensor(y_low[:, t, :], e[:], pages[t][:, :HALF], ADD)
 
-        def add_high(c):
+        def add_low(c):
             cols = slice(c * CHUNK, (c + 1) * CHUNK)
-            for t in range(PACK):
-                nc.vector.tensor_tensor(y_high[c - 2][:, t, :], e_part(c, t), pages[t][:, cols], ADD)
-            nc.sync.dma_start(out=out_rows[:, :, cols], in_=y_high[c - 2][:])
+            for t in range(2, PACK):
+                nc.vector.tensor_tensor(y_low[:, t, cols], e_part(c, t), pages[t][:, cols], ADD)
+            nc.sync.dma_start(out=out_rows[:, 1:, cols], in_=y_low[:, 1:, cols])
 
-        def hand_on(c):
+        def add_high(y_high, c):
+            cols = slice(c * CHUNK, (c + 1) * CHUNK)
+            y = y_high[:, :, c * CHUNK - HALF : (c + 1) * CHUNK - HALF]
+            for t in range(PACK):
+                nc.vector.tensor_tensor(y[:, t, :], e_part(c, t), pages[t][:, cols], ADD)
+                if t % 2:
+                    nc.sync.dma_start(out=out_rows[:, t - 1 : t + 1, cols], in_=y[:, t - 1 : t + 1, :])
+
+        def hand_on(y_half, c):
             cols = slice(c * CHUNK, (c + 1) * CHUNK)
             y_bf = sbuf("y_bf%d" % c, [P, CHUNK, PACK], BF16)
-            interleave(nc.vector.tensor_copy if c == CHUNKS - 1 else nc.scalar.copy, y_bf[:],
-                       y_low_by_t[:, :, cols] if c < 2 else y_high[c - 2][:])
-            y_codes = sbuf("y_codes%d" % c, [P, CHUNK], I32)
-            nc.vector.quantize_mx(out=y_codes[:].bitcast(FP8X4), scales=y_scales[:, cols], in_=y_bf[:].rearrange("p c t -> p (c t)"))
-            nc.sync.dma_start(out=out_words[:, cols], in_=y_codes[:])
+            y = y_half[:, :, (c % 2) * CHUNK : (c % 2 + 1) * CHUNK]
+            split = LAST_ON_SCALAR if c == CHUNKS - 1 else CHUNK
+            interleave(nc.scalar.copy, y_bf[:, :split, :], y[:, :, :split])
+            if split < CHUNK:
+                interleave(nc.vector.tensor_copy, y_bf[:, split:, :], y[:, :, split:])
+            nc.vector.quantize_mx(out=y_codes[:, cols].bitcast(FP8X4), scales=y_scales[:, cols], in_=y_bf[:].rearrange("p c t -> p (c t)"))
 
-        exit_product(0)
-        exit_product(1)
-        place(0)
-        place(1)
-        add_low(0, HALF)
-        place(2)
-        add_low(1, HALF)
-        exit_product(2)
-        add_low(2, HALF)
-        place(3)
-        add_low(3, CHUNK)
-        exit_product(3)
-        add_high(2)
-        hand_on(0)
-        add_high(3)
-        for c in range(1, CHUNKS):
-            hand_on(c)
+        def store_codes(first, last):
+            cols = slice(first * CHUNK, (last + 1) * CHUNK)
+            nc.sync.dma_start(out=out_words[:, cols], in_=y_codes[:, cols])
+
+        exit_product([e[:] for e in e_low], *quantise("low", low_bf, HALF))
+        for t in range(PACK):
+            place(t)
+        rounded2 = round_high(2, "wb_codes")
+        add_low_on_gpsimd(0)
+        nc.sync.dma_start(out=out_rows[:, 0, :HALF], in_=y_low[:, 0, :])
+        add_low_on_gpsimd(1)
+        rounded3 = round_high(3, "low_codes")
+        exit_high(2, rounded2)
+        add_low(0)
+        add_low(1)
+        exit_high(3, rounded3)
+        y_high = sbuf("y_high", [P, PACK, HALF], F32, tag="e_copy1")
+        add_high(y_high, 2)
+        hand_on(y_low, 0)
+        store_codes(0, 0)
+        add_high(y_high, 3)
+        hand_on(y_low, 1)
+        hand_on(y_high, 2)
+        store_codes(1, 2)
+        hand_on(y_high, 3)
+        store_codes(3, 3)
         out_scales = out_2[0].bitcast(I32)
         for q in range(QUADS):
             queues[1 - q % 2].dma_start(out=out_scales[4 * q : 4 * q + 4, :], in_=y_scales[:].bitcast(I32)[32 * q : 32 * q + 4, :])

from contextlib import ExitStack

import concourse.mybir as mybir

K, T, J, R, N = 512, 1024, 128, 512, 512
FLOPS = 2 * K * R * T + 2 * R * N * T + 2 * R * N * J

F32 = mybir.dt.float32
BF16 = mybir.dt.bfloat16
I32 = mybir.dt.int32
U16 = mybir.dt.uint16
U8 = mybir.dt.uint8
FP8X4 = mybir.dt.float8_e4m3fn_x4
FP4X4 = mybir.dt.float4_e2m1fn_x4
RELU = mybir.ActivationFunctionType.Relu
ADD = mybir.AluOpType.add
MAX = mybir.AluOpType.max

P = 128
PACK = 4
QUADS = 4
HALF = 512
CHUNK = 256
CHUNKS = T // CHUNK
LAST_ON_SCALAR = 96
VECTOR_BANKS = (1, 3, 6)


def interleave(copy, dst, src):
    copy(out=dst.rearrange("p (c i) t -> p c t i", i=4), in_=src.rearrange("p t (c i) -> p c t i", i=4))


def deal(nc, dst, src, run):
    nc.vector.tensor_copy(out=dst.rearrange("p t (c i) -> p c t i", i=run), in_=src.rearrange("p (c i) t -> p c t i", i=run))


def tile_list_stay_or_leave_pl_kernel(tc, xq_words, xq_scales, w1_words, w1_scales, wx_words, wx_scales,
                                          wb_words, wb_scales, offs, out_0, out_1, out_2):
    nc = tc.nc
    with ExitStack() as ctx:
        keep = ctx.enter_context(tc.tile_pool(name="keep", bufs=1))
        psum = ctx.enter_context(tc.psum_pool(name="psum", bufs=1))

        def sbuf(name, shape, dtype, tag=None):
            return keep.tile(shape, dtype, name=name, tag=tag or name, align_bytes=64)

        def bank(name, index, shape):
            return psum.tile(shape, F32, name=name, tag="bank%d" % index)

        offsets = keep.tile([P, J // 16], U16, name="offsets")

        w1_raw = sbuf("w1_raw", [P, R], I32)
        w1s_raw = sbuf("w1s_raw", [P, R], U8)
        x_codes = sbuf("x_codes", [P, 2 * T], U8)
        x_scales = sbuf("x_scales", [P, T], U8)
        wb_raw = sbuf("wb_raw", [P, N], I32)
        wx_raw = sbuf("wx_raw", [P, N], U16)
        second_raw = sbuf("second_raw", [P, N], U8)
        nc.vector.memset(second_raw[:].bitcast(I32), 0)

        pages = [sbuf("page%d" % t, [P, T], F32) for t in range(PACK)]
        for t in range(PACK):
            (nc.gpsimd if t == 3 else nc.vector).memset(pages[t][:].bitcast(I32), 0)

        def load_plane(queue, plane, scales, q):
            rows = scales[0].bitcast(I32)[4 * q : 4 * q + 4, :]
            queue.dma_start(out=plane[:].bitcast(I32)[32 * q : 32 * q + 32, :], in_=rows.partition_broadcast(8))

        def load_rows(queue, first, scales, q):
            rows = scales[0].bitcast(I32)[4 * q : 4 * q + 4, :]
            queue.dma_start(out=second_raw[:].bitcast(I32)[32 * q + first : 32 * q + first + 4, :], in_=rows)

        def words(ap):
            return ap[0].rearrange("p n t -> p (n t)").bitcast(I32)

        queues = (nc.sync, nc.scalar)
        for q in range(QUADS):
            load_plane(queues[q % 2], w1s_raw, w1_scales, q)
        nc.sync.dma_start(out=w1_raw[:], in_=words(w1_words))
        nc.scalar.dma_start(out=x_codes[:].bitcast(I32), in_=xq_words[0].bitcast(I32))
        for q in range(QUADS):
            if q == 2:
                warm = sbuf("warm", [P, 1], F32)
                nc.scalar.activation(warm[:], pages[0][:, :1], RELU)
            load_plane(queues[q % 2], x_scales, xq_scales, q)
        nc.sync.dma_start(offsets[:], offs)
        nc.sync.dma_start(out=wb_raw[:], in_=words(wb_words))
        nc.scalar.dma_start(out=wx_raw[:].bitcast(I32), in_=wx_words[0].bitcast(I32))
        for q in range(QUADS):
            load_rows(queues[1 - q % 2], 4, wb_scales, q)
        for q in range(QUADS):
            load_rows(queues[1 - q % 2], 0, wx_scales, q)

        w1_first = sbuf("w1_first", [P, 1, P], I32)
        w1s_first = sbuf("w1s_first", [P, 1, P], U8)
        w1_rest = sbuf("w1_rest", [P, PACK - 1, P], I32)
        w1s_rest = sbuf("w1s_rest", [P, PACK - 1, P], U8)
        w1_by_t = w1_raw[:].rearrange("p (m t) -> p m t", t=PACK)
        w1s_by_t = w1s_raw[:].rearrange("p (m t) -> p m t", t=PACK)
        deal(nc, w1s_first[:], w1s_by_t[:, :, :1], 16)
        deal(nc, w1_first[:], w1_by_t[:, :, :1], 4)
        deal(nc, w1s_rest[:], w1s_by_t[:, :, 1:], 16)
        deal(nc, w1_rest[:], w1_by_t[:, :, 1:], 4)
        w1_codes = [w1_first[:, 0, :]] + [w1_rest[:, t, :] for t in range(PACK - 1)]
        w1_planes = [w1s_first[:, 0, :]] + [w1s_rest[:, t, :] for t in range(PACK - 1)]

        wb_codes = sbuf("wb_codes", [P, PACK, P], I32)
        wx_codes = sbuf("wx_codes", [P, PACK, P], U16)
        second_planes = sbuf("second_planes", [P, PACK, P], U8)

        hid = sbuf("hid", [P, PACK * T], F32)
        low_bf = sbuf("low_bf", [P, HALF, PACK], BF16)
        picked = low_bf[:, :J, :]
        for t in range(PACK):
            for h in range(2):
                b = 2 * t + h
                a = bank("a%d" % b, b, [P, HALF])
                nc.tensor.matmul_mx(out=a[:], lhsT=w1_codes[t].bitcast(FP8X4), lhsT_scale=w1_planes[t],
                                    rhs=x_codes[:, 2 * h * HALF : 2 * (h + 1) * HALF].bitcast(FP4X4), rhs_scale=x_scales[:, h * HALF : (h + 1) * HALF],
                                    start=True, stop=True)
                dst = hid[:, b * HALF : (b + 1) * HALF]
                if b in VECTOR_BANKS:
                    nc.vector.tensor_scalar_max(dst, a[:], 0.0)
                else:
                    nc.scalar.activation(dst, a[:], RELU)
            nc.vector.tensor_copy(picked[:, :, t], hid[:, t * T : (t + 1) * T].indirect(offsets[:]))

        deal(nc, wb_codes[:], wb_raw[:].rearrange("p (m t) -> p m t", t=PACK), 4)
        deal(nc, wx_codes[:], wx_raw[:].rearrange("p (m t) -> p m t", t=PACK), 8)
        deal(nc, second_planes[:], second_raw[:].rearrange("p (m t) -> p m t", t=PACK), 16)

        picked_codes = sbuf("picked_codes", [P, J], I32)
        picked_scales = sbuf("picked_scales", [P, J], U8)
        nc.vector.quantize_mx(out=picked_codes[:].bitcast(FP8X4), scales=picked_scales[:],
                              in_=picked.rearrange("p j t -> p (j t)"))
        p_first = bank("p_first", 0, [P, 1, J])
        p_rest = bank("p_rest", 1, [P, PACK - 1, J])
        p_slices = [p_first[:, 0, :]] + [p_rest[:, t, :] for t in range(PACK - 1)]
        for t in range(PACK):
            nc.tensor.matmul_mx(out=p_slices[t], lhsT=wb_codes[:, t, :].bitcast(FP8X4), lhsT_scale=second_planes[4:, t, :],
                                rhs=picked_codes[:].bitcast(FP8X4), rhs_scale=picked_scales[:], start=True, stop=True)
        d = [sbuf("d%d" % t, [P, J], F32) for t in range(PACK)]
        hid_by_t = hid[:].rearrange("p (t c) -> p t c", t=PACK)

        def round_hid(copy, dst, first, count):
            interleave(copy, dst, hid_by_t[:, :, first : first + count])

        def quantise(name, rounded, width, tag=None):
            codes = sbuf(name + "_codes", [P, width], I32, tag=tag)
            scales = sbuf(name + "_scales", [P, width], U8)
            nc.vector.quantize_mx(out=codes[:].bitcast(FP8X4), scales=scales[:], in_=rounded[:].rearrange("p c t -> p (c t)"))
            return codes, scales

        def exit_product(e_slices, codes, scales):
            for t in range(PACK):
                nc.tensor.matmul_mx(out=e_slices[t], lhsT=wx_codes[:, t, :].bitcast(FP4X4), lhsT_scale=second_planes[:, t, :],
                                    rhs=codes[:].bitcast(FP8X4), rhs_scale=scales[:], start=True, stop=True)

        for first in range(J, HALF, J):
            round_hid(nc.scalar.copy, low_bf[:, first : first + J, :], first, J)
        for t in range(PACK):
            nc.scalar.activation(d[t][:], p_slices[t], RELU, scale=4.0)
        round_hid(nc.vector.tensor_copy, picked, 0, J)

        e_low = [bank("e_low%d" % t, 2 + t, [P, HALF]) for t in range(PACK)]
        e_high = [bank("e_high%d" % u, (6 + u) % 8, [P, 2, CHUNK]) for u in range(PACK)]

        def e_part(c, t):
            return e_low[t][:, c * CHUNK : (c + 1) * CHUNK] if c < 2 else e_high[2 * (c - 2) + t // 2][:, t % 2, :]

        def round_high(c, tag):
            rounded = sbuf("hid_bf%d" % c, [P, CHUNK, PACK], BF16, tag=tag)
            for first in range(0, CHUNK, J):
                round_hid(nc.scalar.copy, rounded[:, first : first + J, :], c * CHUNK + first, J)
            return rounded

        def exit_high(c, rounded):
            exit_product([e_part(c, t) for t in range(PACK)], *quantise("hid%d" % c, rounded, CHUNK))

        out_rows = out_0.rearrange("(p t) c -> p t c", t=PACK)
        out_words = words(out_1)
        y_low = sbuf("y_low", [P, PACK, HALF], F32)
        y_codes = sbuf("y_codes", [P, T], I32)
        y_scales = sbuf("y_scales", [P, T], U8)

        def place(t):
            nc.vector.tensor_copy(pages[t][:].indirect(offsets[:]), d[t][:])

        def add_low_on_gpsimd(t):
            e = sbuf("e_copy%d" % t, [P, HALF], F32)
            nc.scalar.copy(e[:], e_low[t][:])
            nc.gpsimd.tensor_tensor(y_low[:, t, :], e[:], pages[t][:, :HALF], ADD)

        def add_low(c):
            cols = slice(c * CHUNK, (c + 1) * CHUNK)
            for t in range(2, PACK):
                nc.vector.tensor_tensor(y_low[:, t, cols], e_part(c, t), pages[t][:, cols], ADD)
            nc.sync.dma_start(out=out_rows[:, 1:, cols], in_=y_low[:, 1:, cols])

        def add_high(y_high, c):
            cols = slice(c * CHUNK, (c + 1) * CHUNK)
            y = y_high[:, :, c * CHUNK - HALF : (c + 1) * CHUNK - HALF]
            for t in range(PACK):
                nc.vector.tensor_tensor(y[:, t, :], e_part(c, t), pages[t][:, cols], ADD)
                if t % 2:
                    nc.sync.dma_start(out=out_rows[:, t - 1 : t + 1, cols], in_=y[:, t - 1 : t + 1, :])

        def hand_on(y_half, c):
            cols = slice(c * CHUNK, (c + 1) * CHUNK)
            y_bf = sbuf("y_bf%d" % c, [P, CHUNK, PACK], BF16)
            y = y_half[:, :, (c % 2) * CHUNK : (c % 2 + 1) * CHUNK]
            split = LAST_ON_SCALAR if c == CHUNKS - 1 else CHUNK
            interleave(nc.scalar.copy, y_bf[:, :split, :], y[:, :, :split])
            if split < CHUNK:
                interleave(nc.vector.tensor_copy, y_bf[:, split:, :], y[:, :, split:])
            nc.vector.quantize_mx(out=y_codes[:, cols].bitcast(FP8X4), scales=y_scales[:, cols], in_=y_bf[:].rearrange("p c t -> p (c t)"))

        def store_codes(first, last):
            cols = slice(first * CHUNK, (last + 1) * CHUNK)
            nc.sync.dma_start(out=out_words[:, cols], in_=y_codes[:, cols])

        exit_product([e[:] for e in e_low], *quantise("low", low_bf, HALF))
        for t in range(PACK):
            place(t)
        rounded2 = round_high(2, "wb_codes")
        add_low_on_gpsimd(0)
        nc.sync.dma_start(out=out_rows[:, 0, :HALF], in_=y_low[:, 0, :])
        add_low_on_gpsimd(1)
        rounded3 = round_high(3, "low_codes")
        exit_high(2, rounded2)
        add_low(0)
        add_low(1)
        exit_high(3, rounded3)
        y_high = sbuf("y_high", [P, PACK, HALF], F32, tag="e_copy1")
        add_high(y_high, 2)
        hand_on(y_low, 0)
        store_codes(0, 0)
        add_high(y_high, 3)
        hand_on(y_low, 1)
        hand_on(y_high, 2)
        store_codes(1, 2)
        hand_on(y_high, 3)
        store_codes(3, 3)
        out_scales = out_2[0].bitcast(I32)
        for q in range(QUADS):
            queues[1 - q % 2].dma_start(out=out_scales[4 * q : 4 * q + 4, :], in_=y_scales[:].bitcast(I32)[32 * q : 32 * q + 4, :])
